import numpy as np
import ml_dtypes


def mxq(x, axis, fmt="e4m3"):
    dtype, down = {"e4m3": (ml_dtypes.float8_e4m3fn, 7), "e5m2": (ml_dtypes.float8_e5m2, 14)}[fmt]
    v = np.moveaxis(np.asarray(x, np.float32).astype(ml_dtypes.bfloat16).astype(np.float64), axis, -1)
    blocks = v.reshape(v.shape[:-1] + (-1, 32))
    amax = np.abs(blocks).max(-1, keepdims=True)
    byte = np.maximum(np.where(amax > 0, np.frexp(amax)[1] - 1 + 127, 0) - down, 1)
    scale = np.exp2(byte - 127.0)
    codes = (blocks / scale).astype(np.float32).astype(dtype).astype(np.float64)
    return np.moveaxis((codes * scale).reshape(v.shape), -1, axis)


WIDE = False


def mx_kscale(k):
    if not WIDE:
        return np.ones(k)
    levels = np.array([10, -10, 5, -5, 0])
    if k % 512:
        return np.exp2(np.random.permutation(np.resize(levels, k // 32))).repeat(32)
    a = np.empty((k // 512, 16))
    for p in range(k // 512):
        a[p, :8] = np.random.permutation(np.resize(levels, 8))
        for g in range(8):
            far = levels[np.abs(levels - a[p, g]) >= 10]
            a[p, g + 8] = far[np.random.randint(len(far))]
    return np.exp2(a.ravel()).repeat(32)


def f64(x):
    return np.asarray(x).astype(np.float64)


def striped(idx):
    return np.tile(idx.reshape(-1, 16).T, (8, 1)).astype(np.uint16)


def unstriped(offs):
    return offs[:16].T.reshape(-1).astype(np.int64)


def striped8(idx):
    return np.concatenate([x.reshape(-1, 16).T for x in idx]).astype(np.uint16)


def runs(offs, k):
    lists = np.stack([offs[16 * r : 16 * r + 16].T.reshape(-1) for r in range(8)]).astype(np.int64)
    return lists[np.arange(k) % 512 // 64]


def pack_weight(w):
    k, n = w.shape
    w = f64(np.asarray(w, np.float32).astype(ml_dtypes.bfloat16)).reshape(k // 32, 32, n)
    amax = np.abs(w).max(1)
    byte = np.clip(np.where(amax > 0, np.frexp(amax)[1] - 1 + 127 - 7, 1), 1, 254)
    scaled = (w * np.exp2(127.0 - byte)[:, None, :]).reshape(k, n).astype(np.float32)
    words = np.ascontiguousarray(scaled.reshape(k // 512, 128, 4, n).transpose(0, 1, 3, 2)).astype(ml_dtypes.float8_e4m3fn).view(np.uint8)
    return words, np.ascontiguousarray(byte.astype(np.uint8).reshape(k // 512, 16, n))


def unpack_weight(words, scales):
    g, p, n, _ = words.shape
    vals = np.ascontiguousarray(words).view(ml_dtypes.float8_e4m3fn).astype(np.float64) * np.repeat(np.exp2(scales.astype(np.float64) - 127.0), 8, axis=1)[..., None]
    return vals.transpose(0, 1, 3, 2).reshape(g * 512, n)


K, T, S, N, H = 512, 2048, 512, 512, 512


def setup_inputs():
    n = np.random.standard_normal
    s = mx_kscale(K)[:, None]
    u = mx_kscale(H)
    packed_xT = pack_weight(n((K, T)) * s)
    return {
        "x_words": packed_xT[0],
        "x_scales": packed_xT[1],
        "w1": (n((K, H)) / np.sqrt(K) / s).astype(np.float32),
        "tau": np.random.uniform(0.5, 1.2, (H, 1)).astype(np.float32),
        "gn": (np.random.uniform(0.5, 1.5, (H, 1)) * u[:, None]).astype(np.float32),
        "w2": (n((H, N)) / np.sqrt(H) / u[:, None]).astype(np.float32),
        "offs": striped(np.random.permutation(T)[:S]),
        "n1": striped(np.random.permutation(S)),
        "n2": striped(np.random.permutation(S)),
        "n3": striped8(np.stack([np.random.permutation(S) for _ in range(8)])),
        "n4": striped8(np.stack([np.random.permutation(S) for _ in range(8)])),
        "n5": striped8(np.stack([np.random.permutation(S) for _ in range(8)])),
    }


def reference(x_words, x_scales, w1, tau, gn, w2, offs, n1, n2, n3, n4, n5):
    xq = unpack_weight(x_words, x_scales)[:, unstriped(offs)]
    y = mxq(f64(w1), 0, "e4m3").T @ xq
    sz = np.abs(y)
    ea = np.exp(-1.0 * (f64(tau) * sz[:, unstriped(n1)]))
    z = f64(gn) * ((y - y[:, unstriped(n2)]) * ea)
    h = mxq(f64(w2), 0, "e4m3").T @ mxq(z, 0, "e4m3")
    return y * (h[np.arange(N)[:, None], runs(n3, N)] - h) + 0.5 * ((y[np.arange(H)[:, None], runs(n5, H)]) * (h[np.arange(N)[:, None], runs(n4, N)] - h))

@@ -1,0 +1,193 @@
+from contextlib import ExitStack
+
+import concourse.mybir as mybir
+
+F32 = mybir.dt.float32
+BF16 = mybir.dt.bfloat16
+I32 = mybir.dt.int32
+U32 = mybir.dt.uint32
+U16 = mybir.dt.uint16
+U8 = mybir.dt.uint8
+FP8X4 = mybir.dt.float8_e4m3fn_x4
+ALU = mybir.AluOpType
+ACT = mybir.ActivationFunctionType
+
+P = 128
+PACK = 4
+K, T, S, H, N = 512, 2048, 512, 512, 512
+HALF = S // 2
+LIST_COLS = S // 16
+RING = 6
+FLOPS = 2 * K * H * S + 2 * H * N * S
+
+
+def tile_picked_skipflowbela_none_p_kernel(
+    tc, x_words, x_scales, w1, tau, gn, w2, offs, n1, n2, n3, n4, n5, out
+):
+    nc = tc.nc
+    with ExitStack() as ctx:
+        lists = ctx.enter_context(tc.tile_pool(name="lists", bufs=1))
+        keep = ctx.enter_context(tc.tile_pool(name="keep", bufs=1))
+        psum = ctx.enter_context(tc.psum_pool(name="psum", bufs=1))
+
+        def cols(half):
+            return slice(half * HALF, (half + 1) * HALF)
+
+        def load_list(src, name):
+            tile = lists.tile([P, LIST_COLS], U16, name=name)
+            nc.sync.dma_start(tile[:], src)
+            return tile
+
+        def half_list(tile, half):
+            return tile[:, half * (LIST_COLS // 2) : (half + 1) * (LIST_COLS // 2)]
+
+        def fetched():
+            return keep.tile([P, HALF], F32, name="fetched", tag="fetched", bufs=RING)
+
+        def load_weight(w):
+            raw = keep.tile([P, PACK, 512], F32, name="w_raw", tag="w_raw")
+            nc.sync.dma_start(raw[:], w.rearrange("(p j) c -> p j c", j=PACK))
+            return raw
+
+        def deal_weight(copy, raw, pair, name):
+            dealt = keep.tile([P, 2, P, PACK], BF16, name=name, align_bytes=64)
+            src = raw[:].rearrange("p j (m t) -> p m j t", t=PACK)[:, :, :, 2 * pair : 2 * pair + 2]
+            copy(dealt[:].rearrange("p t m j -> p m j t"), src)
+            return dealt
+
+        def quantize(src, width, name):
+            codes = keep.tile([P, width], U32, name=name + "_codes", align_bytes=64)
+            scales = keep.tile([P, width], U8, name=name + "_scales", align_bytes=64)
+            nc.vector.quantize_mx(codes[:].bitcast(FP8X4), scales[:], src)
+            return codes, scales
+
+        def product(dst, w_q, t, codes, scales):
+            w_codes, w_scales = w_q[t // 2]
+            m = slice((t % 2) * P, (t % 2 + 1) * P)
+            nc.tensor.matmul_mx(
+                dst,
+                lhsT=w_codes[:, m].bitcast(FP8X4),
+                lhsT_scale=w_scales[:, m],
+                rhs=codes.bitcast(FP8X4),
+                rhs_scale=scales,
+                start=True,
+                stop=True,
+            )
+
+        scale_table = keep.tile([P, T], U8, name="scale_table", align_bytes=64)
+        nc.vector.memset(scale_table[:].bitcast(I32), 0)
+        offs_t = load_list(offs, "offs_t")
+        n2_t = load_list(n2, "n2_t")
+        n1_t = load_list(n1, "n1_t")
+        n5_t = load_list(n5, "n5_t")
+        w1_raw = load_weight(w1)
+        word_table = keep.tile([P, T], I32, name="word_table", align_bytes=64)
+        nc.sync.dma_start(word_table[:], x_words[0].rearrange("p c r -> p (c r)").bitcast(I32))
+        for q in range(4):
+            nc.scalar.dma_start(
+                scale_table[32 * q : 32 * q + 4, :].bitcast(I32),
+                x_scales[0, 4 * q : 4 * q + 4, :].bitcast(I32),
+            )
+        tau_t = keep.tile([P, PACK], F32, name="tau_t")
+        nc.gpsimd.dma_start(tau_t[:], tau.rearrange("(p t) o -> p (t o)", t=PACK))
+        gn_t = keep.tile([P, PACK], F32, name="gn_t")
+        nc.gpsimd.dma_start(gn_t[:], gn.rearrange("(p t) o -> p (t o)", t=PACK))
+        n3_t = load_list(n3, "n3_t")
+        n4_t = load_list(n4, "n4_t")
+        neg_tau = keep.tile([P, PACK], F32, name="neg_tau")
+        nc.gpsimd.tensor_scalar(neg_tau[:], tau_t[:], -1.0, 0.0, ALU.mult, ALU.add)
+
+        picked_scales = keep.tile([P, S], U8, name="picked_scales", align_bytes=64)
+        nc.vector.tensor_copy(picked_scales[:], scale_table[:].indirect(offs_t[:]))
+        w1_dealt = [
+            deal_weight(nc.scalar.copy, w1_raw, 0, "w1_dealt0"),
+            deal_weight(nc.vector.tensor_copy, w1_raw, 1, "w1_dealt1"),
+        ]
+        w2_raw = load_weight(w2)
+        w1_q = [None, None]
+        for pair in (1, 0):
+            w1_q[pair] = quantize(w1_dealt[pair][:].rearrange("p t m j -> p (t m j)"), 2 * P, "w1_%d" % pair)
+        picked_words = []
+        for half in range(2):
+            words = keep.tile([P, HALF], U32, name="picked_words%d" % half, align_bytes=64)
+            nc.vector.tensor_copy(words[:], word_table[:].bitcast(U32).indirect(half_list(offs_t, half)))
+            picked_words.append(words)
+
+        y_ps = [psum.tile([P, S], F32, name="y_ps%d" % t) for t in range(PACK)]
+        h_ps = [psum.tile([P, S], F32, name="h_ps%d" % t) for t in range(PACK)]
+        for t in range(PACK):
+            for half in range(2):
+                product(y_ps[t][:, cols(half)], w1_q, t, picked_words[half][:], picked_scales[:, cols(half)])
+
+        y_sb, sz = [], []
+        for t in range(PACK):
+            y_t = keep.tile([P, S], F32, name="y_sb%d" % t)
+            sz_t = keep.tile([P, S], F32, name="sz%d" % t)
+            nc.vector.tensor_copy(y_t[:], y_ps[t][:])
+            if t == 0:
+                nc.vector.scalar_tensor_tensor(sz_t[:], y_ps[t][:], -1.0, y_t[:], ALU.mult, ALU.max)
+            else:
+                nc.scalar.activation(sz_t[:], y_t[:], ACT.Abs)
+            y_sb.append(y_t)
+            sz.append(sz_t)
+
+        w2_dealt, w2_q = [], []
+        for half in range(2):
+            z = keep.tile([P, PACK, HALF], BF16, name="z%d" % half)
+            for t in range(PACK):
+                y2 = fetched()
+                ea = fetched()
+                d = keep.tile([P, HALF], F32, name="d_%d_%d" % (half, t))
+                nc.scalar.activation(y2[:], y_sb[t][:].indirect(half_list(n2_t, half)), ACT.Copy)
+                nc.scalar.activation(
+                    ea[:], sz[t][:].indirect(half_list(n1_t, half)), ACT.Exp, scale=neg_tau[:, t : t + 1]
+                )
+                if half == 0 and t < 2:
+                    w2_dealt.append(deal_weight(nc.vector.tensor_copy, w2_raw, t, "w2_dealt%d" % t))
+                if half == 0 and t in (1, 2):
+                    w2_q.append(quantize(w2_dealt[t - 1][:].rearrange("p t m j -> p (t m j)"), 2 * P, "w2_%d" % t))
+                nc.vector.tensor_tensor(d[:], y_ps[t][:, cols(half)], y2[:], ALU.subtract)
+                nc.vector.scalar_tensor_tensor(z[:, t, :], d[:], gn_t[:, t : t + 1], ea[:], ALU.mult, ALU.mult)
+            z_il = keep.tile([P, HALF, PACK], BF16, name="z_il%d" % half, align_bytes=64)
+            nc.vector.tensor_copy(
+                z_il[:].rearrange("p (c i) t -> p c t i", i=4),
+                z[:].rearrange("p t (c i) -> p c t i", i=4),
+            )
+            z_codes, z_scales = quantize(z_il[:].rearrange("p c t -> p (c t)"), HALF, "zq%d" % half)
+            for t in range(PACK):
+                product(h_ps[t][:, cols(half)], w2_q, t, z_codes[:], z_scales[:])
+
+        out_rows = out.rearrange("(p t) n -> p t n", t=PACK)
+        for t in range(PACK):
+            h_t = keep.tile([P, S], F32, name="h_sb%d" % t)
+            if t == 0:
+                h_plain = keep.tile([P, S], F32, name="h_plain")
+                for half in range(2):
+                    nc.vector.tensor_copy(h_t[:, cols(half)], h_ps[t][:, cols(half)])
+                nc.vector.tensor_copy(h_plain[:], h_t[:])
+            else:
+                nc.scalar.copy(h_t[:], h_ps[t][:])
+            for half in range(2):
+                c = cols(half)
+                tag = "_%d_%d" % (t, half)
+                d3 = keep.tile([P, HALF], F32, name="d3" + tag)
+                d4 = keep.tile([P, HALF], F32, name="d4" + tag)
+                e = keep.tile([P, HALF], F32, name="e" + tag)
+                f = keep.tile([P, HALF], F32, name="f" + tag)
+                res = keep.tile([P, HALF], F32, name="res" + tag)
+                if t == 0:
+                    nc.vector.tensor_tensor(d3[:], h_t[:].indirect(half_list(n3_t, half)), h_plain[:, c], ALU.subtract)
+                    nc.vector.tensor_tensor(d4[:], h_t[:].indirect(half_list(n4_t, half)), h_plain[:, c], ALU.subtract)
+                else:
+                    h3 = fetched()
+                    h4 = fetched()
+                    nc.scalar.activation(h3[:], h_t[:].indirect(half_list(n3_t, half)), ACT.Copy)
+                    nc.scalar.activation(h4[:], h_t[:].indirect(half_list(n4_t, half)), ACT.Copy)
+                    nc.vector.tensor_tensor(d3[:], h3[:], h_ps[t][:, c], ALU.subtract)
+                    nc.vector.tensor_tensor(d4[:], h4[:], h_ps[t][:, c], ALU.subtract)
+                y5 = fetched()
+                nc.scalar.activation(y5[:], y_sb[t][:].indirect(half_list(n5_t, half)), ACT.Copy)
+                nc.vector.tensor_tensor(e[:], d3[:], y_ps[t][:, c], ALU.mult)
+                nc.vector.scalar_tensor_tensor(f[:], d4[:], 0.5, y5[:], ALU.mult, ALU.mult)
+                nc.vector.tensor_tensor(res[:], e[:], f[:], ALU.add)
+                nc.sync.dma_start(out_rows[:, t, c], res[:])

@@ -17,7 +17,6 @@ PACK = 4
 K, T, S, H, N = 512, 2048, 512, 512, 512
 HALF = S // 2
 LIST_COLS = S // 16
-RING = 6
 FLOPS = 2 * K * H * S + 2 * H * N * S
 
 
@@ -40,9 +39,6 @@ def tile_picked_skipflowbela_none_p_kernel(
 
         def half_list(tile, half):
             return tile[:, half * (LIST_COLS // 2) : (half + 1) * (LIST_COLS // 2)]
-
-        def fetched():
-            return keep.tile([P, HALF], F32, name="fetched", tag="fetched", bufs=RING)
 
         def load_weight(w):
             raw = keep.tile([P, PACK, 512], F32, name="w_raw", tag="w_raw")
@@ -119,75 +115,125 @@ def tile_picked_skipflowbela_none_p_kernel(
             for half in range(2):
                 product(y_ps[t][:, cols(half)], w1_q, t, picked_words[half][:], picked_scales[:, cols(half)])
 
-        y_sb, sz = [], []
-        for t in range(PACK):
-            y_t = keep.tile([P, S], F32, name="y_sb%d" % t)
-            sz_t = keep.tile([P, S], F32, name="sz%d" % t)
-            nc.vector.tensor_copy(y_t[:], y_ps[t][:])
-            if t == 0:
-                nc.vector.scalar_tensor_tensor(sz_t[:], y_ps[t][:], -1.0, y_t[:], ALU.mult, ALU.max)
-            else:
-                nc.scalar.activation(sz_t[:], y_t[:], ACT.Abs)
-            y_sb.append(y_t)
-            sz.append(sz_t)
+        y_sb = [keep.tile([P, S], F32, name="y_sb%d" % t) for t in range(PACK)]
+        sz = [keep.tile([P, S], F32, name="sz%d" % t) for t in range(PACK)]
+        for pair in range(2):
+            for t in (2 * pair, 2 * pair + 1):
+                nc.vector.tensor_copy(y_sb[t][:], y_ps[t][:])
+            t = 2 * pair
+            nc.vector.scalar_tensor_tensor(sz[t][:], y_ps[t][:], -1.0, y_sb[t][:], ALU.mult, ALU.max)
 
-        w2_dealt, w2_q = [], []
+        w2_dealt = []
+        for pair in range(2):
+            dealt = keep.tile([P, 2, P, PACK], BF16, name="w2_dealt%d" % pair, align_bytes=64)
+            src = w2_raw[:].rearrange("p j (m t) -> p t m j", t=PACK)[:, 2 * pair : 2 * pair + 2, :, :]
+            nc.gpsimd.tensor_scalar(dealt[:], src, 1.0, 0.0, ALU.mult, ALU.add)
+            w2_dealt.append(dealt)
+
+        h_sb = [keep.tile([P, S], F32, name="h_sb%d" % t) for t in range(PACK)]
+        h_plain = keep.tile([P, S], F32, name="h_plain")
+        w2_q = []
         for half in range(2):
             z = keep.tile([P, PACK, HALF], BF16, name="z%d" % half)
-            for t in range(PACK):
-                y2 = fetched()
-                ea = fetched()
-                d = keep.tile([P, HALF], F32, name="d_%d_%d" % (half, t))
-                nc.scalar.activation(y2[:], y_sb[t][:].indirect(half_list(n2_t, half)), ACT.Copy)
-                nc.scalar.activation(
-                    ea[:], sz[t][:].indirect(half_list(n1_t, half)), ACT.Exp, scale=neg_tau[:, t : t + 1]
-                )
-                if half == 0 and t < 2:
-                    w2_dealt.append(deal_weight(nc.vector.tensor_copy, w2_raw, t, "w2_dealt%d" % t))
-                if half == 0 and t in (1, 2):
-                    w2_q.append(quantize(w2_dealt[t - 1][:].rearrange("p t m j -> p (t m j)"), 2 * P, "w2_%d" % t))
-                nc.vector.tensor_tensor(d[:], y_ps[t][:, cols(half)], y2[:], ALU.subtract)
-                nc.vector.scalar_tensor_tensor(z[:, t, :], d[:], gn_t[:, t : t + 1], ea[:], ALU.mult, ALU.mult)
+            for pair in range(2):
+                both = (2 * pair, 2 * pair + 1)
+                y2, ea, d = {}, {}, {}
+                for t in both:
+                    y2[t] = keep.tile([P, HALF], F32, name="y2", tag="y2_%d" % t)
+                    if half == 0 and t % 2 == 1:
+                        nc.scalar.activation(sz[t][:], y_sb[t][:], ACT.Abs)
+                    nc.scalar.activation(y2[t][:], y_sb[t][:].indirect(half_list(n2_t, half)), ACT.Copy)
+                for t in both:
+                    ea[t] = keep.tile([P, HALF], F32, name="ea", tag="ea_%d" % t)
+                    nc.scalar.activation(
+                        ea[t][:], sz[t][:].indirect(half_list(n1_t, half)), ACT.Exp, scale=neg_tau[:, t : t + 1]
+                    )
+                for t in both:
+                    d[t] = keep.tile([P, HALF], F32, name="d_%d_%d" % (half, t))
+                    nc.vector.tensor_tensor(d[t][:], y_ps[t][:, cols(half)], y2[t][:], ALU.subtract)
+                for t in both:
+                    nc.vector.scalar_tensor_tensor(z[:, t, :], d[t][:], gn_t[:, t : t + 1], ea[t][:], ALU.mult, ALU.mult)
+                if half == 0 and pair == 1:
+                    for k in range(2):
+                        w2_q.append(quantize(w2_dealt[k][:].rearrange("p t m j -> p (t m j)"), 2 * P, "w2_%d" % k))
+            if half == 1:
+                nc.vector.tensor_copy(h_sb[0][:, cols(0)], h_ps[0][:, cols(0)])
             z_il = keep.tile([P, HALF, PACK], BF16, name="z_il%d" % half, align_bytes=64)
             nc.vector.tensor_copy(
                 z_il[:].rearrange("p (c i) t -> p c t i", i=4),
                 z[:].rearrange("p t (c i) -> p c t i", i=4),
             )
+            if half == 1:
+                nc.vector.tensor_copy(h_plain[:, cols(0)], h_ps[0][:, cols(0)])
             z_codes, z_scales = quantize(z_il[:].rearrange("p c t -> p (c t)"), HALF, "zq%d" % half)
             for t in range(PACK):
+                if half == 1 and t == 1:
+                    nc.vector.tensor_copy(h_sb[t][:, cols(0)], h_ps[t][:, cols(0)])
                 product(h_ps[t][:, cols(half)], w2_q, t, z_codes[:], z_scales[:])
 
         out_rows = out.rearrange("(p t) n -> p t n", t=PACK)
-        for t in range(PACK):
-            h_t = keep.tile([P, S], F32, name="h_sb%d" % t)
-            if t == 0:
-                h_plain = keep.tile([P, S], F32, name="h_plain")
-                for half in range(2):
-                    nc.vector.tensor_copy(h_t[:, cols(half)], h_ps[t][:, cols(half)])
-                nc.vector.tensor_copy(h_plain[:], h_t[:])
+
+        def fetch(engine, dst, table, offsets, half):
+            window = table[:].indirect(half_list(offsets, half))
+            if engine == "vector":
+                nc.vector.tensor_copy(dst[:, cols(half)], window)
             else:
-                nc.scalar.copy(h_t[:], h_ps[t][:])
+                nc.scalar.activation(dst[:, cols(half)], window, ACT.Copy)
+
+        def fetch_half_y5(dst, t, half):
+            nc.scalar.activation(dst[:, cols(half)], y_sb[t][:].indirect(half_list(n5_t, half)), ACT.Copy, scale=0.5)
+
+        y5 = {}
+        for t in range(2):
+            y5[t] = keep.tile([P, S], F32, name="y5", tag="y2_%d" % (2 + t))
             for half in range(2):
-                c = cols(half)
-                tag = "_%d_%d" % (t, half)
-                d3 = keep.tile([P, HALF], F32, name="d3" + tag)
-                d4 = keep.tile([P, HALF], F32, name="d4" + tag)
-                e = keep.tile([P, HALF], F32, name="e" + tag)
-                f = keep.tile([P, HALF], F32, name="f" + tag)
-                res = keep.tile([P, HALF], F32, name="res" + tag)
-                if t == 0:
-                    nc.vector.tensor_tensor(d3[:], h_t[:].indirect(half_list(n3_t, half)), h_plain[:, c], ALU.subtract)
-                    nc.vector.tensor_tensor(d4[:], h_t[:].indirect(half_list(n4_t, half)), h_plain[:, c], ALU.subtract)
-                else:
-                    h3 = fetched()
-                    h4 = fetched()
-                    nc.scalar.activation(h3[:], h_t[:].indirect(half_list(n3_t, half)), ACT.Copy)
-                    nc.scalar.activation(h4[:], h_t[:].indirect(half_list(n4_t, half)), ACT.Copy)
-                    nc.vector.tensor_tensor(d3[:], h3[:], h_ps[t][:, c], ALU.subtract)
-                    nc.vector.tensor_tensor(d4[:], h4[:], h_ps[t][:, c], ALU.subtract)
-                y5 = fetched()
-                nc.scalar.activation(y5[:], y_sb[t][:].indirect(half_list(n5_t, half)), ACT.Copy)
-                nc.vector.tensor_tensor(e[:], d3[:], y_ps[t][:, c], ALU.mult)
-                nc.vector.scalar_tensor_tensor(f[:], d4[:], 0.5, y5[:], ALU.mult, ALU.mult)
-                nc.vector.tensor_tensor(res[:], e[:], f[:], ALU.add)
-                nc.sync.dma_start(out_rows[:, t, c], res[:])
+                fetch_half_y5(y5[t], t, half)
+        for t in range(PACK):
+            d3 = keep.tile([P, S], F32, name="d3_%d" % t)
+            d4 = keep.tile([P, S], F32, name="d4_%d" % t)
+            e = keep.tile([P, S], F32, name="e_%d" % t)
+            f = keep.tile([P, S], F32, name="f_%d" % t)
+            res = keep.tile([P, S], F32, name="res_%d" % t)
+            if t == 0:
+                nc.vector.tensor_copy(h_sb[t][:, cols(1)], h_ps[t][:, cols(1)])
+                nc.vector.tensor_copy(h_plain[:, cols(1)], h_ps[t][:, cols(1)])
+                for dst, offsets in ((d4, n4_t), (d3, n3_t)):
+                    for half in range(2):
+                        c = cols(half)
+                        nc.vector.tensor_tensor(
+                            dst[:, c], h_sb[t][:].indirect(half_list(offsets, half)), h_plain[:, c], ALU.subtract
+                        )
+            else:
+                h3 = keep.tile([P, S], F32, name="h3_%d" % t)
+                h4 = keep.tile([P, S], F32, name="h4_%d" % t)
+                rest = cols(1) if t == 1 else slice(0, S)
+                nc.scalar.copy(h_sb[t][:, rest], h_ps[t][:, rest])
+                if t > 1:
+                    y5[t] = keep.tile([P, S], F32, name="y5", tag="y2_%d" % t)
+            if t in (1, 2):
+                for half in range(2):
+                    fetch("vector" if t == 1 else "scalar", h4, h_sb[t], n4_t, half)
+                if t == 2:
+                    for half in range(2):
+                        fetch_half_y5(y5[t], t, half)
+                for half in range(2):
+                    fetch("scalar", h3, h_sb[t], n3_t, half)
+                nc.vector.tensor_tensor(d4[:], h4[:], h_ps[t][:], ALU.subtract)
+                nc.vector.tensor_tensor(d3[:], h3[:], h_ps[t][:], ALU.subtract)
+            if t < PACK - 1:
+                nc.gpsimd.tensor_tensor(f[:], d4[:], y5[t][:], ALU.mult)
+                nc.vector.tensor_tensor(e[:], d3[:], y_ps[t][:], ALU.mult)
+                nc.gpsimd.tensor_tensor(res[:], e[:], f[:], ALU.add)
+                nc.sync.dma_start(out_rows[:, t, :], res[:])
+            else:
+                for half in range(2):
+                    c = cols(half)
+                    fetch("scalar", h3, h_sb[t], n3_t, half)
+                    fetch("scalar", h4, h_sb[t], n4_t, half)
+                    fetch_half_y5(y5[t], t, half)
+                    nc.vector.tensor_tensor(d3[:, c], h3[:, c], h_ps[t][:, c], ALU.subtract)
+                    nc.vector.tensor_tensor(d4[:, c], h4[:, c], h_ps[t][:, c], ALU.subtract)
+                    nc.vector.tensor_tensor(e[:, c], d3[:, c], y_ps[t][:, c], ALU.mult)
+                    nc.vector.tensor_tensor(f[:, c], d4[:, c], y5[t][:, c], ALU.mult)
+                    nc.vector.tensor_tensor(res[:, c], e[:, c], f[:, c], ALU.add)
+                    nc.sync.dma_start(out_rows[:, t, c], res[:, c])

@@ -93,6 +93,13 @@ def tile_picked_skipflowbela_none_p_kernel(
         neg_tau = keep.tile([P, PACK], F32, name="neg_tau")
         nc.gpsimd.tensor_scalar(neg_tau[:], tau_t[:], -1.0, 0.0, ALU.mult, ALU.add)
 
+        y_win = [keep.tile([P, 2 * S if t < 3 else S], F32, name="y_win%d" % t) for t in range(PACK)]
+        sz_win = [keep.tile([P, 2 * S if t < 2 else S], F32, name="sz_win%d" % t) for t in range(PACK)]
+        for t in range(2):
+            nc.vector.memset(y_win[t][:, S:], 0.0)
+        y_sb = [tile[:, :S] for tile in y_win]
+        sz = [tile[:, :S] for tile in sz_win]
+
         picked_scales = keep.tile([P, S], U8, name="picked_scales", align_bytes=64)
         nc.vector.tensor_copy(picked_scales[:], scale_table[:].indirect(offs_t[:]))
         w1_dealt = [
@@ -115,13 +122,11 @@ def tile_picked_skipflowbela_none_p_kernel(
             for half in range(2):
                 product(y_ps[t][:, cols(half)], w1_q, t, picked_words[half][:], picked_scales[:, cols(half)])
 
-        y_sb = [keep.tile([P, S], F32, name="y_sb%d" % t) for t in range(PACK)]
-        sz = [keep.tile([P, S], F32, name="sz%d" % t) for t in range(PACK)]
         for pair in range(2):
             for t in (2 * pair, 2 * pair + 1):
-                nc.vector.tensor_copy(y_sb[t][:], y_ps[t][:])
-            t = 2 * pair
-            nc.vector.scalar_tensor_tensor(sz[t][:], y_ps[t][:], -1.0, y_sb[t][:], ALU.mult, ALU.max)
+                nc.vector.tensor_copy(y_sb[t], y_ps[t][:])
+            for t in (2 * pair, 2 * pair + 1):
+                nc.vector.scalar_tensor_tensor(sz[t], y_ps[t][:], -1.0, y_sb[t], ALU.mult, ALU.max)
 
         w2_dealt = []
         for pair in range(2):
@@ -130,110 +135,114 @@ def tile_picked_skipflowbela_none_p_kernel(
             nc.gpsimd.tensor_scalar(dealt[:], src, 1.0, 0.0, ALU.mult, ALU.add)
             w2_dealt.append(dealt)
 
-        h_sb = [keep.tile([P, S], F32, name="h_sb%d" % t) for t in range(PACK)]
-        h_plain = keep.tile([P, S], F32, name="h_plain")
-        w2_q = []
-        for half in range(2):
-            z = keep.tile([P, PACK, HALF], BF16, name="z%d" % half)
-            for pair in range(2):
-                both = (2 * pair, 2 * pair + 1)
-                y2, ea, d = {}, {}, {}
-                for t in both:
-                    y2[t] = keep.tile([P, HALF], F32, name="y2", tag="y2_%d" % t)
-                    if half == 0 and t % 2 == 1:
-                        nc.scalar.activation(sz[t][:], y_sb[t][:], ACT.Abs)
-                    nc.scalar.activation(y2[t][:], y_sb[t][:].indirect(half_list(n2_t, half)), ACT.Copy)
-                for t in both:
-                    ea[t] = keep.tile([P, HALF], F32, name="ea", tag="ea_%d" % t)
-                    nc.scalar.activation(
-                        ea[t][:], sz[t][:].indirect(half_list(n1_t, half)), ACT.Exp, scale=neg_tau[:, t : t + 1]
-                    )
-                for t in both:
-                    d[t] = keep.tile([P, HALF], F32, name="d_%d_%d" % (half, t))
-                    nc.vector.tensor_tensor(d[t][:], y_ps[t][:, cols(half)], y2[t][:], ALU.subtract)
-                for t in both:
-                    nc.vector.scalar_tensor_tensor(z[:, t, :], d[t][:], gn_t[:, t : t + 1], ea[t][:], ALU.mult, ALU.mult)
-                if half == 0 and pair == 1:
-                    for k in range(2):
-                        w2_q.append(quantize(w2_dealt[k][:].rearrange("p t m j -> p (t m j)"), 2 * P, "w2_%d" % k))
-            if half == 1:
-                nc.vector.tensor_copy(h_sb[0][:, cols(0)], h_ps[0][:, cols(0)])
+        def entries(tile, c):
+            return tile[:, c.start // 16 : c.stop // 16]
+
+        z = keep.tile([P, PACK, S], BF16, name="z")
+
+        def make_z(both, c):
+            width = c.stop - c.start
+            y2, ea, d = {}, {}, {}
+            for t in both:
+                if t < 2:
+                    y2[t] = sz_win[t][:, S:]
+                else:
+                    y2[t] = keep.tile([P, width], F32, name="y2", tag="y2_%d" % t)[:]
+                nc.scalar.activation(y2[t], y_win[t][:].indirect(entries(n2_t, c)), ACT.Copy)
+            for t in both:
+                if t == 0:
+                    ea[t] = y_win[2][:, S:]
+                else:
+                    ea[t] = keep.tile([P, width], F32, name="ea", tag="ea_%d" % t)[:]
+                nc.scalar.activation(
+                    ea[t], sz_win[t][:].indirect(entries(n1_t, c)), ACT.Exp, scale=neg_tau[:, t : t + 1]
+                )
+            for t in both:
+                d[t] = keep.tile([P, width], F32, name="d_%d_%d" % (c.start, t))
+                nc.vector.tensor_tensor(d[t][:], y_ps[t][:, c], y2[t], ALU.subtract)
+            for t in both:
+                nc.vector.scalar_tensor_tensor(z[:, t, c], d[t][:], gn_t[:, t : t + 1], ea[t], ALU.mult, ALU.mult)
+
+        def weave_z(half):
             z_il = keep.tile([P, HALF, PACK], BF16, name="z_il%d" % half, align_bytes=64)
             nc.vector.tensor_copy(
                 z_il[:].rearrange("p (c i) t -> p c t i", i=4),
-                z[:].rearrange("p t (c i) -> p c t i", i=4),
+                z[:, :, cols(half)].rearrange("p t (c i) -> p c t i", i=4),
             )
-            if half == 1:
-                nc.vector.tensor_copy(h_plain[:, cols(0)], h_ps[0][:, cols(0)])
-            z_codes, z_scales = quantize(z_il[:].rearrange("p c t -> p (c t)"), HALF, "zq%d" % half)
-            for t in range(PACK):
-                if half == 1 and t == 1:
-                    nc.vector.tensor_copy(h_sb[t][:, cols(0)], h_ps[t][:, cols(0)])
-                product(h_ps[t][:, cols(half)], w2_q, t, z_codes[:], z_scales[:])
+            return z_il[:].rearrange("p c t -> p (c t)")
+
+        whole = slice(0, S)
+        make_z((0, 1), whole)
+        w2_q = [quantize(w2_dealt[k][:].rearrange("p t m j -> p (t m j)"), 2 * P, "w2_%d" % k) for k in range(2)]
+        make_z((2, 3), cols(0))
+        z_codes, z_scales = quantize(weave_z(0), HALF, "zq0")
+        for t in range(PACK):
+            product(h_ps[t][:, cols(0)], w2_q, t, z_codes[:], z_scales[:])
+        make_z((2, 3), cols(1))
+
+        h_win = [keep.tile([P, 2 * S], F32, name="h_win", tag=tag) for tag in ("y2_2", "y2_3", "ea_3")]
+        h_win.append(keep.tile([P, S], F32, name="h_win3"))
+        y5 = [tile[:, S:] for tile in h_win[:3]]
+
+        def fetch_half_y5(t, c):
+            nc.scalar.activation(y5[t][:, c], y_win[t][:].indirect(entries(n5_t, c)), ACT.Copy, scale=0.5)
+
+        def unload_h(t, c):
+            nc.vector.tensor_copy(h_win[t][:, c], h_ps[t][:, c])
+
+        for t in range(3):
+            fetch_half_y5(t, whole)
+        unload_h(0, cols(0))
+        woven = weave_z(1)
+        unload_h(1, cols(0))
+        z_codes, z_scales = quantize(woven, HALF, "zq1")
+        for t in range(PACK):
+            product(h_ps[t][:, cols(1)], w2_q, t, z_codes[:], z_scales[:])
 
         out_rows = out.rearrange("(p t) n -> p t n", t=PACK)
 
-        def fetch(engine, dst, table, offsets, half):
-            window = table[:].indirect(half_list(offsets, half))
-            if engine == "vector":
-                nc.vector.tensor_copy(dst[:, cols(half)], window)
-            else:
-                nc.scalar.activation(dst[:, cols(half)], window, ACT.Copy)
+        def work(name):
+            return [keep.tile([P, S], F32, name="%s_%d" % (name, t)) for t in range(PACK)]
 
-        def fetch_half_y5(dst, t, half):
-            nc.scalar.activation(dst[:, cols(half)], y_sb[t][:].indirect(half_list(n5_t, half)), ACT.Copy, scale=0.5)
+        def fetch_h(dst, t, offsets, c):
+            nc.scalar.activation(dst[t][:, c], h_win[t][:].indirect(entries(offsets, c)), ACT.Copy)
 
-        y5 = {}
-        for t in range(2):
-            y5[t] = keep.tile([P, S], F32, name="y5", tag="y2_%d" % (2 + t))
-            for half in range(2):
-                fetch_half_y5(y5[t], t, half)
-        for t in range(PACK):
-            d3 = keep.tile([P, S], F32, name="d3_%d" % t)
-            d4 = keep.tile([P, S], F32, name="d4_%d" % t)
-            e = keep.tile([P, S], F32, name="e_%d" % t)
-            f = keep.tile([P, S], F32, name="f_%d" % t)
-            res = keep.tile([P, S], F32, name="res_%d" % t)
+        def less_h(dst, fetched, t, c):
+            nc.vector.tensor_tensor(dst[t][:, c], fetched[t][:, c], h_ps[t][:, c], ALU.subtract)
+
+        def times_y(t, c):
+            nc.vector.tensor_tensor(e[t][:, c], d3[t][:, c], y_ps[t][:, c], ALU.mult)
+
+        h3, h4, d3, d4, e, f, res = [work(name) for name in ("h3", "h4", "d3", "d4", "e", "f", "res")]
+        unload_h(0, cols(1))
+        unload_h(1, cols(1))
+        for t in range(3):
             if t == 0:
-                nc.vector.tensor_copy(h_sb[t][:, cols(1)], h_ps[t][:, cols(1)])
-                nc.vector.tensor_copy(h_plain[:, cols(1)], h_ps[t][:, cols(1)])
-                for dst, offsets in ((d4, n4_t), (d3, n3_t)):
-                    for half in range(2):
-                        c = cols(half)
-                        nc.vector.tensor_tensor(
-                            dst[:, c], h_sb[t][:].indirect(half_list(offsets, half)), h_plain[:, c], ALU.subtract
-                        )
+                nc.vector.tensor_copy(h4[t][:], h_win[t][:].indirect(n4_t[:]))
             else:
-                h3 = keep.tile([P, S], F32, name="h3_%d" % t)
-                h4 = keep.tile([P, S], F32, name="h4_%d" % t)
-                rest = cols(1) if t == 1 else slice(0, S)
-                nc.scalar.copy(h_sb[t][:, rest], h_ps[t][:, rest])
-                if t > 1:
-                    y5[t] = keep.tile([P, S], F32, name="y5", tag="y2_%d" % t)
-            if t in (1, 2):
-                for half in range(2):
-                    fetch("vector" if t == 1 else "scalar", h4, h_sb[t], n4_t, half)
-                if t == 2:
-                    for half in range(2):
-                        fetch_half_y5(y5[t], t, half)
-                for half in range(2):
-                    fetch("scalar", h3, h_sb[t], n3_t, half)
-                nc.vector.tensor_tensor(d4[:], h4[:], h_ps[t][:], ALU.subtract)
-                nc.vector.tensor_tensor(d3[:], h3[:], h_ps[t][:], ALU.subtract)
-            if t < PACK - 1:
-                nc.gpsimd.tensor_tensor(f[:], d4[:], y5[t][:], ALU.mult)
-                nc.vector.tensor_tensor(e[:], d3[:], y_ps[t][:], ALU.mult)
-                nc.gpsimd.tensor_tensor(res[:], e[:], f[:], ALU.add)
-                nc.sync.dma_start(out_rows[:, t, :], res[:])
-            else:
-                for half in range(2):
-                    c = cols(half)
-                    fetch("scalar", h3, h_sb[t], n3_t, half)
-                    fetch("scalar", h4, h_sb[t], n4_t, half)
-                    fetch_half_y5(y5[t], t, half)
-                    nc.vector.tensor_tensor(d3[:, c], h3[:, c], h_ps[t][:, c], ALU.subtract)
-                    nc.vector.tensor_tensor(d4[:, c], h4[:, c], h_ps[t][:, c], ALU.subtract)
-                    nc.vector.tensor_tensor(e[:, c], d3[:, c], y_ps[t][:, c], ALU.mult)
-                    nc.vector.tensor_tensor(f[:, c], d4[:, c], y5[t][:, c], ALU.mult)
-                    nc.vector.tensor_tensor(res[:, c], e[:, c], f[:, c], ALU.add)
-                    nc.sync.dma_start(out_rows[:, t, c], res[:, c])
+                fetch_h(h4, t, n4_t, whole)
+            fetch_h(h3, t, n3_t, whole)
+            less_h(d4, h4, t, whole)
+            less_h(d3, h3, t, whole)
+            if t < 2:
+                unload_h(t + 2, whole)
+            times_y(t, whole)
+            nc.gpsimd.tensor_tensor(f[t][:], d4[t][:], y5[t], ALU.mult)
+            nc.gpsimd.tensor_tensor(res[t][:], e[t][:], f[t][:], ALU.add)
+            nc.sync.dma_start(out_rows[:, t, :], res[t][:])
+        t = PACK - 1
+        y5.append(keep.tile([P, S], F32, name="y5_3", tag="y2_2")[:])
+        for half in range(2):
+            c = cols(half)
+            fetch_h(h3, t, n3_t, c)
+            fetch_h(h4, t, n4_t, c)
+            fetch_half_y5(t, c)
+            less_h(d3, h3, t, c)
+            less_h(d4, h4, t, c)
+            times_y(t, c)
+        for half in range(2):
+            nc.vector.tensor_tensor(f[t][:, cols(half)], d4[t][:, cols(half)], y5[t][:, cols(half)], ALU.mult)
+        for half in range(2):
+            c = cols(half)
+            nc.vector.tensor_tensor(res[t][:, c], e[t][:, c], f[t][:, c], ALU.add)
+            nc.sync.dma_start(out_rows[:, t, c], res[t][:, c])

@@ -17,6 +17,7 @@ PACK = 4
 K, T, S, H, N = 512, 2048, 512, 512, 512
 HALF = S // 2
 LIST_COLS = S // 16
+LAST = PACK - 1
 FLOPS = 2 * K * H * S + 2 * H * N * S
 
 
@@ -37,11 +38,11 @@ def tile_picked_skipflowbela_none_p_kernel(
             nc.sync.dma_start(tile[:], src)
             return tile
 
-        def half_list(tile, half):
-            return tile[:, half * (LIST_COLS // 2) : (half + 1) * (LIST_COLS // 2)]
+        def entries(tile, c):
+            return tile[:, c.start // 16 : c.stop // 16]
 
         def load_weight(w):
-            raw = keep.tile([P, PACK, 512], F32, name="w_raw", tag="w_raw")
+            raw = keep.tile([P, PACK, H], F32, name="w_raw", tag="w_raw")
             nc.sync.dma_start(raw[:], w.rearrange("(p j) c -> p j c", j=PACK))
             return raw
 
@@ -93,7 +94,7 @@ def tile_picked_skipflowbela_none_p_kernel(
         neg_tau = keep.tile([P, PACK], F32, name="neg_tau")
         nc.gpsimd.tensor_scalar(neg_tau[:], tau_t[:], -1.0, 0.0, ALU.mult, ALU.add)
 
-        y_win = [keep.tile([P, 2 * S if t < 3 else S], F32, name="y_win%d" % t) for t in range(PACK)]
+        y_win = [keep.tile([P, 2 * S if t < LAST else S], F32, name="y_win%d" % t) for t in range(PACK)]
         sz_win = [keep.tile([P, 2 * S if t < 2 else S], F32, name="sz_win%d" % t) for t in range(PACK)]
         for t in range(2):
             nc.vector.memset(y_win[t][:, S:], 0.0)
@@ -113,7 +114,7 @@ def tile_picked_skipflowbela_none_p_kernel(
         picked_words = []
         for half in range(2):
             words = keep.tile([P, HALF], U32, name="picked_words%d" % half, align_bytes=64)
-            nc.vector.tensor_copy(words[:], word_table[:].bitcast(U32).indirect(half_list(offs_t, half)))
+            nc.vector.tensor_copy(words[:], word_table[:].bitcast(U32).indirect(entries(offs_t, cols(half))))
             picked_words.append(words)
 
         y_ps = [psum.tile([P, S], F32, name="y_ps%d" % t) for t in range(PACK)]
@@ -134,9 +135,6 @@ def tile_picked_skipflowbela_none_p_kernel(
             src = w2_raw[:].rearrange("p j (m t) -> p t m j", t=PACK)[:, 2 * pair : 2 * pair + 2, :, :]
             nc.gpsimd.tensor_scalar(dealt[:], src, 1.0, 0.0, ALU.mult, ALU.add)
             w2_dealt.append(dealt)
-
-        def entries(tile, c):
-            return tile[:, c.start // 16 : c.stop // 16]
 
         z = keep.tile([P, PACK, S], BF16, name="z")
 
@@ -182,16 +180,16 @@ def tile_picked_skipflowbela_none_p_kernel(
 
         h_win = [keep.tile([P, 2 * S], F32, name="h_win", tag=tag) for tag in ("y2_2", "y2_3", "ea_3")]
         h_win.append(keep.tile([P, S], F32, name="h_win3"))
-        y5 = [tile[:, S:] for tile in h_win[:3]]
+        y5 = [tile[:, S:] for tile in h_win[:LAST]]
 
-        def fetch_half_y5(t, c):
-            nc.scalar.activation(y5[t][:, c], y_win[t][:].indirect(entries(n5_t, c)), ACT.Copy, scale=0.5)
+        def fetch_y5(dst, t, c):
+            nc.scalar.activation(dst, y_win[t][:].indirect(entries(n5_t, c)), ACT.Copy, scale=0.5)
 
         def unload_h(t, c):
             nc.vector.tensor_copy(h_win[t][:, c], h_ps[t][:, c])
 
-        for t in range(3):
-            fetch_half_y5(t, whole)
+        for t in range(LAST):
+            fetch_y5(y5[t], t, whole)
         unload_h(0, cols(0))
         woven = weave_z(1)
         unload_h(1, cols(0))
@@ -205,44 +203,49 @@ def tile_picked_skipflowbela_none_p_kernel(
             return [keep.tile([P, S], F32, name="%s_%d" % (name, t)) for t in range(PACK)]
 
         def fetch_h(dst, t, offsets, c):
-            nc.scalar.activation(dst[t][:, c], h_win[t][:].indirect(entries(offsets, c)), ACT.Copy)
+            nc.scalar.activation(dst, h_win[t][:].indirect(entries(offsets, c)), ACT.Copy)
 
         def less_h(dst, fetched, t, c):
-            nc.vector.tensor_tensor(dst[t][:, c], fetched[t][:, c], h_ps[t][:, c], ALU.subtract)
+            nc.vector.tensor_tensor(dst[t][:, c], fetched, h_ps[t][:, c], ALU.subtract)
 
         def times_y(t, c):
             nc.vector.tensor_tensor(e[t][:, c], d3[t][:, c], y_ps[t][:, c], ALU.mult)
 
-        h3, h4, d3, d4, e, f, res = [work(name) for name in ("h3", "h4", "d3", "d4", "e", "f", "res")]
+        h4, d3, d4, e, f, res = [work(name) for name in ("h4", "d3", "d4", "e", "f", "res")]
+        h3 = [keep.tile([P, S], F32, name="h3_%d" % t) for t in range(LAST)]
         unload_h(0, cols(1))
         unload_h(1, cols(1))
-        for t in range(3):
+        for t in range(LAST):
             if t == 0:
                 nc.vector.tensor_copy(h4[t][:], h_win[t][:].indirect(n4_t[:]))
             else:
-                fetch_h(h4, t, n4_t, whole)
-            fetch_h(h3, t, n3_t, whole)
-            less_h(d4, h4, t, whole)
-            less_h(d3, h3, t, whole)
-            if t < 2:
+                fetch_h(h4[t][:], t, n4_t, whole)
+            fetch_h(h3[t][:], t, n3_t, whole)
+            less_h(d4, h4[t][:], t, whole)
+            less_h(d3, h3[t][:], t, whole)
+            if t + 2 < PACK:
                 unload_h(t + 2, whole)
             times_y(t, whole)
             nc.gpsimd.tensor_tensor(f[t][:], d4[t][:], y5[t], ALU.mult)
             nc.gpsimd.tensor_tensor(res[t][:], e[t][:], f[t][:], ALU.add)
             nc.sync.dma_start(out_rows[:, t, :], res[t][:])
-        t = PACK - 1
-        y5.append(keep.tile([P, S], F32, name="y5_3", tag="y2_2")[:])
+
+        y5_last = []
         for half in range(2):
             c = cols(half)
-            fetch_h(h3, t, n3_t, c)
-            fetch_h(h4, t, n4_t, c)
-            fetch_half_y5(t, c)
-            less_h(d3, h3, t, c)
-            less_h(d4, h4, t, c)
-            times_y(t, c)
-        for half in range(2):
-            nc.vector.tensor_tensor(f[t][:, cols(half)], d4[t][:, cols(half)], y5[t][:, cols(half)], ALU.mult)
+            h3_half = keep.tile([P, HALF], F32, name="h3_last", tag="h3_last%d" % half)
+            fetch_h(h3_half[:], LAST, n3_t, c)
+            fetch_h(h4[LAST][:, c], LAST, n4_t, c)
+            less_h(d3, h3_half[:], LAST, c)
+            y5_half = keep.tile([P, HALF], F32, name="y5_last", tag=("y2_2", "h3_last0")[half])
+            fetch_y5(y5_half[:], LAST, c)
+            y5_last.append(y5_half)
+            less_h(d4, h4[LAST][:, c], LAST, c)
+            times_y(LAST, c)
         for half in range(2):
             c = cols(half)
-            nc.vector.tensor_tensor(res[t][:, c], e[t][:, c], f[t][:, c], ALU.add)
-            nc.sync.dma_start(out_rows[:, t, c], res[t][:, c])
+            nc.vector.tensor_tensor(f[LAST][:, c], d4[LAST][:, c], y5_last[half][:], ALU.mult)
+        for half in range(2):
+            c = cols(half)
+            nc.vector.tensor_tensor(res[LAST][:, c], e[LAST][:, c], f[LAST][:, c], ALU.add)
+            nc.sync.dma_start(out_rows[:, LAST, c], res[LAST][:, c])

from contextlib import ExitStack

import concourse.mybir as mybir

F32 = mybir.dt.float32
BF16 = mybir.dt.bfloat16
I32 = mybir.dt.int32
U32 = mybir.dt.uint32
U16 = mybir.dt.uint16
U8 = mybir.dt.uint8
FP8X4 = mybir.dt.float8_e4m3fn_x4
ALU = mybir.AluOpType
ACT = mybir.ActivationFunctionType

P = 128
PACK = 4
K, T, S, H, N = 512, 2048, 512, 512, 512
HALF = S // 2
LIST_COLS = S // 16
LAST = PACK - 1
FLOPS = 2 * K * H * S + 2 * H * N * S


def tile_picked_skipflowbela_none_p_kernel(
    tc, x_words, x_scales, w1, tau, gn, w2, offs, n1, n2, n3, n4, n5, out
):
    nc = tc.nc
    with ExitStack() as ctx:
        lists = ctx.enter_context(tc.tile_pool(name="lists", bufs=1))
        keep = ctx.enter_context(tc.tile_pool(name="keep", bufs=1))
        psum = ctx.enter_context(tc.psum_pool(name="psum", bufs=1))

        def cols(half):
            return slice(half * HALF, (half + 1) * HALF)

        def load_list(src, name):
            tile = lists.tile([P, LIST_COLS], U16, name=name)
            nc.sync.dma_start(tile[:], src)
            return tile

        def entries(tile, c):
            return tile[:, c.start // 16 : c.stop // 16]

        def load_weight(w):
            raw = keep.tile([P, PACK, H], F32, name="w_raw", tag="w_raw")
            nc.sync.dma_start(raw[:], w.rearrange("(p j) c -> p j c", j=PACK))
            return raw

        def deal_weight(copy, raw, pair, name):
            dealt = keep.tile([P, 2, P, PACK], BF16, name=name, align_bytes=64)
            src = raw[:].rearrange("p j (m t) -> p m j t", t=PACK)[:, :, :, 2 * pair : 2 * pair + 2]
            copy(dealt[:].rearrange("p t m j -> p m j t"), src)
            return dealt

        def quantize(src, width, name):
            codes = keep.tile([P, width], U32, name=name + "_codes", align_bytes=64)
            scales = keep.tile([P, width], U8, name=name + "_scales", align_bytes=64)
            nc.vector.quantize_mx(codes[:].bitcast(FP8X4), scales[:], src)
            return codes, scales

        def product(dst, w_q, t, codes, scales):
            w_codes, w_scales = w_q[t // 2]
            m = slice((t % 2) * P, (t % 2 + 1) * P)
            nc.tensor.matmul_mx(
                dst,
                lhsT=w_codes[:, m].bitcast(FP8X4),
                lhsT_scale=w_scales[:, m],
                rhs=codes.bitcast(FP8X4),
                rhs_scale=scales,
                start=True,
                stop=True,
            )

        scale_table = keep.tile([P, T], U8, name="scale_table", align_bytes=64)
        nc.vector.memset(scale_table[:].bitcast(I32), 0)
        offs_t = load_list(offs, "offs_t")
        n2_t = load_list(n2, "n2_t")
        n1_t = load_list(n1, "n1_t")
        n5_t = load_list(n5, "n5_t")
        w1_raw = load_weight(w1)
        word_table = keep.tile([P, T], I32, name="word_table", align_bytes=64)
        nc.sync.dma_start(word_table[:], x_words[0].rearrange("p c r -> p (c r)").bitcast(I32))
        for q in range(4):
            nc.scalar.dma_start(
                scale_table[32 * q : 32 * q + 4, :].bitcast(I32),
                x_scales[0, 4 * q : 4 * q + 4, :].bitcast(I32),
            )
        tau_t = keep.tile([P, PACK], F32, name="tau_t")
        nc.gpsimd.dma_start(tau_t[:], tau.rearrange("(p t) o -> p (t o)", t=PACK))
        gn_t = keep.tile([P, PACK], F32, name="gn_t")
        nc.gpsimd.dma_start(gn_t[:], gn.rearrange("(p t) o -> p (t o)", t=PACK))
        n3_t = load_list(n3, "n3_t")
        n4_t = load_list(n4, "n4_t")
        neg_tau = keep.tile([P, PACK], F32, name="neg_tau")
        nc.gpsimd.tensor_scalar(neg_tau[:], tau_t[:], -1.0, 0.0, ALU.mult, ALU.add)

        y_win = [keep.tile([P, 2 * S if t < LAST else S], F32, name="y_win%d" % t) for t in range(PACK)]
        sz_win = [keep.tile([P, 2 * S if t < 2 else S], F32, name="sz_win%d" % t) for t in range(PACK)]
        for t in range(2):
            nc.vector.memset(y_win[t][:, S:], 0.0)
        y_sb = [tile[:, :S] for tile in y_win]
        sz = [tile[:, :S] for tile in sz_win]

        picked_scales = keep.tile([P, S], U8, name="picked_scales", align_bytes=64)
        nc.vector.tensor_copy(picked_scales[:], scale_table[:].indirect(offs_t[:]))
        w1_dealt = [
            deal_weight(nc.scalar.copy, w1_raw, 0, "w1_dealt0"),
            deal_weight(nc.vector.tensor_copy, w1_raw, 1, "w1_dealt1"),
        ]
        w2_raw = load_weight(w2)
        w1_q = [None, None]
        for pair in (1, 0):
            w1_q[pair] = quantize(w1_dealt[pair][:].rearrange("p t m j -> p (t m j)"), 2 * P, "w1_%d" % pair)
        picked_words = []
        for half in range(2):
            words = keep.tile([P, HALF], U32, name="picked_words%d" % half, align_bytes=64)
            nc.vector.tensor_copy(words[:], word_table[:].bitcast(U32).indirect(entries(offs_t, cols(half))))
            picked_words.append(words)

        y_ps = [psum.tile([P, S], F32, name="y_ps%d" % t) for t in range(PACK)]
        h_ps = [psum.tile([P, S], F32, name="h_ps%d" % t) for t in range(PACK)]
        for t in range(PACK):
            for half in range(2):
                product(y_ps[t][:, cols(half)], w1_q, t, picked_words[half][:], picked_scales[:, cols(half)])

        for pair in range(2):
            for t in (2 * pair, 2 * pair + 1):
                nc.vector.tensor_copy(y_sb[t], y_ps[t][:])
            for t in (2 * pair, 2 * pair + 1):
                nc.vector.scalar_tensor_tensor(sz[t], y_ps[t][:], -1.0, y_sb[t], ALU.mult, ALU.max)

        w2_dealt = []
        for pair in range(2):
            dealt = keep.tile([P, 2, P, PACK], BF16, name="w2_dealt%d" % pair, align_bytes=64)
            src = w2_raw[:].rearrange("p j (m t) -> p t m j", t=PACK)[:, 2 * pair : 2 * pair + 2, :, :]
            nc.gpsimd.tensor_scalar(dealt[:], src, 1.0, 0.0, ALU.mult, ALU.add)
            w2_dealt.append(dealt)

        z = keep.tile([P, PACK, S], BF16, name="z")

        def make_z(both, c):
            width = c.stop - c.start
            y2, ea, d = {}, {}, {}
            for t in both:
                if t < 2:
                    y2[t] = sz_win[t][:, S:]
                else:
                    y2[t] = keep.tile([P, width], F32, name="y2", tag="y2_%d" % t)[:]
                nc.scalar.activation(y2[t], y_win[t][:].indirect(entries(n2_t, c)), ACT.Copy)
            for t in both:
                if t == 0:
                    ea[t] = y_win[2][:, S:]
                else:
                    ea[t] = keep.tile([P, width], F32, name="ea", tag="ea_%d" % t)[:]
                nc.scalar.activation(
                    ea[t], sz_win[t][:].indirect(entries(n1_t, c)), ACT.Exp, scale=neg_tau[:, t : t + 1]
                )
            for t in both:
                d[t] = keep.tile([P, width], F32, name="d_%d_%d" % (c.start, t))
                nc.vector.tensor_tensor(d[t][:], y_ps[t][:, c], y2[t], ALU.subtract)
            for t in both:
                nc.vector.scalar_tensor_tensor(z[:, t, c], d[t][:], gn_t[:, t : t + 1], ea[t], ALU.mult, ALU.mult)

        def weave_z(half):
            z_il = keep.tile([P, HALF, PACK], BF16, name="z_il%d" % half, align_bytes=64)
            nc.vector.tensor_copy(
                z_il[:].rearrange("p (c i) t -> p c t i", i=4),
                z[:, :, cols(half)].rearrange("p t (c i) -> p c t i", i=4),
            )
            return z_il[:].rearrange("p c t -> p (c t)")

        whole = slice(0, S)
        make_z((0, 1), whole)
        w2_q = [quantize(w2_dealt[k][:].rearrange("p t m j -> p (t m j)"), 2 * P, "w2_%d" % k) for k in range(2)]
        make_z((2, 3), cols(0))
        z_codes, z_scales = quantize(weave_z(0), HALF, "zq0")
        for t in range(PACK):
            product(h_ps[t][:, cols(0)], w2_q, t, z_codes[:], z_scales[:])
        make_z((2, 3), cols(1))

        h_win = [keep.tile([P, 2 * S], F32, name="h_win", tag=tag) for tag in ("y2_2", "y2_3", "ea_3")]
        h_win.append(keep.tile([P, S], F32, name="h_win3"))
        y5 = [tile[:, S:] for tile in h_win[:LAST]]

        def fetch_y5(dst, t, c):
            nc.scalar.activation(dst, y_win[t][:].indirect(entries(n5_t, c)), ACT.Copy, scale=0.5)

        def unload_h(t, c):
            nc.vector.tensor_copy(h_win[t][:, c], h_ps[t][:, c])

        for t in range(LAST):
            fetch_y5(y5[t], t, whole)
        unload_h(0, cols(0))
        woven = weave_z(1)
        unload_h(1, cols(0))
        z_codes, z_scales = quantize(woven, HALF, "zq1")
        for t in range(PACK):
            product(h_ps[t][:, cols(1)], w2_q, t, z_codes[:], z_scales[:])

        out_rows = out.rearrange("(p t) n -> p t n", t=PACK)

        def work(name):
            return [keep.tile([P, S], F32, name="%s_%d" % (name, t)) for t in range(PACK)]

        def fetch_h(dst, t, offsets, c):
            nc.scalar.activation(dst, h_win[t][:].indirect(entries(offsets, c)), ACT.Copy)

        def less_h(dst, fetched, t, c):
            nc.vector.tensor_tensor(dst[t][:, c], fetched, h_ps[t][:, c], ALU.subtract)

        def times_y(t, c):
            nc.vector.tensor_tensor(e[t][:, c], d3[t][:, c], y_ps[t][:, c], ALU.mult)

        h4, d3, d4, e, f, res = [work(name) for name in ("h4", "d3", "d4", "e", "f", "res")]
        h3 = [keep.tile([P, S], F32, name="h3_%d" % t) for t in range(LAST)]
        unload_h(0, cols(1))
        unload_h(1, cols(1))
        for t in range(LAST):
            if t == 0:
                nc.vector.tensor_copy(h4[t][:], h_win[t][:].indirect(n4_t[:]))
            else:
                fetch_h(h4[t][:], t, n4_t, whole)
            fetch_h(h3[t][:], t, n3_t, whole)
            less_h(d4, h4[t][:], t, whole)
            less_h(d3, h3[t][:], t, whole)
            if t + 2 < PACK:
                unload_h(t + 2, whole)
            times_y(t, whole)
            nc.gpsimd.tensor_tensor(f[t][:], d4[t][:], y5[t], ALU.mult)
            nc.gpsimd.tensor_tensor(res[t][:], e[t][:], f[t][:], ALU.add)
            nc.sync.dma_start(out_rows[:, t, :], res[t][:])

        y5_last = []
        for half in range(2):
            c = cols(half)
            h3_half = keep.tile([P, HALF], F32, name="h3_last", tag="h3_last%d" % half)
            fetch_h(h3_half[:], LAST, n3_t, c)
            fetch_h(h4[LAST][:, c], LAST, n4_t, c)
            less_h(d3, h3_half[:], LAST, c)
            y5_half = keep.tile([P, HALF], F32, name="y5_last", tag=("y2_2", "h3_last0")[half])
            fetch_y5(y5_half[:], LAST, c)
            y5_last.append(y5_half)
            less_h(d4, h4[LAST][:, c], LAST, c)
            times_y(LAST, c)
        for half in range(2):
            c = cols(half)
            nc.vector.tensor_tensor(f[LAST][:, c], d4[LAST][:, c], y5_last[half][:], ALU.mult)
        for half in range(2):
            c = cols(half)
            nc.vector.tensor_tensor(res[LAST][:, c], e[LAST][:, c], f[LAST][:, c], ALU.add)
            nc.sync.dma_start(out_rows[:, LAST, c], res[LAST][:, c])
